import numpy as np
CORES = [3,11,19,27,35,43,51,59,67,75,83,91,99,107,115,123,131,139,147,155,163,171,179,187,195,203,211,219,227,235,243,251]
N = 32
DEAD = {"mate_links":[[4,0],[4,1],[18,0],[26,1]],"switch_ports":[[9,1],[30,0]],"chips":[]}
def setup_inputs(rng):
    return {"x": rng.standard_normal((N, 128, 512), dtype=np.float32)}
def reference(x):
    b = 512 // N
    blocks = x.reshape(N, 128, N, b)
    return {"y": np.ascontiguousarray(blocks.transpose(2, 1, 0, 3)).reshape(N, 128, 512)}

@@ -1,0 +1,141 @@
+import math
+from concourse.bass import DstId, RemoteDMATransfer
+
+N = 32
+B = 16
+RANK_CORE = 3
+
+SCRATCH = {
+    "xs": ("sbuf", [128, 512], "float32"),
+    "land": ("sbuf", [128, 512], "float32"),
+}
+SEMAPHORES = ["loaded", "arrived", "sent", "stored"]
+
+CACHE = {}
+
+
+def plan(dead, topo):
+    dead_mate = {(c & ~1, d) for c, d in dead["mate_links"]}
+    dead_port = {(c, d) for c, d in dead["switch_ports"]}
+
+    def way(a, die, b):
+        links, cur = [], a
+        if (a ^ b) & 1:
+            if (cur & ~1, die) in dead_mate:
+                return None
+            links.append(("mate", cur, die))
+            cur ^= 1
+        if cur != b:
+            if (cur, die) in dead_port or (b, die) in dead_port:
+                return None
+            links.append(("out", cur, die))
+            links.append(("in", b, die))
+        return links
+
+    def candidates(s, d):
+        out = []
+        for die in (1, 0):
+            w = way(s, die, d)
+            if w is not None:
+                out.append(((s, die), w + [("leave", s), ("enter", d)] + ([("die0", s)] if die == 0 else [])))
+        for m in range(N):
+            if m in (s, d) or (s // 16 == d // 16 and m // 16 != s // 16):
+                continue
+            w1 = way(s, 1, m)
+            if w1 is None:
+                continue
+            for die in (1, 0):
+                w2 = way(m, die, d)
+                if w2 is not None:
+                    out.append(((m, die), w1 + w2 + [("leave", s), ("enter", m), ("leave", m), ("enter", d), ("relayed", s)]))
+        return out
+
+    cand = {(s, d): candidates(s, d) for s in range(N) for d in range(N) if s != d}
+    cap = {"leave": 33, "enter": 33, "out": 30, "in": 30, "mate": 16, "die0": 16, "relayed": 16}
+    load = {}
+
+    def cost(res):
+        c = 0.0
+        for r in res:
+            n, k = load.get(r, 0) + 1, cap[r[0]]
+            c += (n / k) ** 6 + (1000.0 * (n - k) if n > k else 0.0)
+        return c
+
+    keys = sorted(cand, key=lambda k: (len(cand[k]), k))
+    choice = {}
+    for sweep in range(12):
+        for k in keys:
+            if k in choice:
+                for r in cand[k][choice[k]][1]:
+                    load[r] -= 1
+            choice[k] = min(range(len(cand[k])), key=lambda i: (cost(cand[k][i][1]), i))
+            for r in cand[k][choice[k]][1]:
+                load[r] = load.get(r, 0) + 1
+
+    direct = {s: 0 for s in range(N)}
+    jobs = {}
+    sends, inbound = {}, {}
+    for (s, d) in keys:
+        m, die = cand[(s, d)][choice[(s, d)]][0]
+        if m != s:
+            direct[s] += 1
+    hop = []
+    for (s, d) in sorted(keys):
+        m, die = cand[(s, d)][choice[(s, d)]][0]
+        if m == s and die == 1 and direct[s] < 16:
+            direct[s] += 1
+            sends.setdefault(8 * s + RANK_CORE, []).append((8 * d + RANK_CORE, d, s))
+        else:
+            hop.append(((m ^ d) & 1 == 0, s, d, m, die))
+    work = {}
+    for same, s, d, m, die in sorted(hop):
+        pool = [c for c in range(8 * m, 8 * m + 8) if c % 8 != RANK_CORE and topo.die(c) == die
+                and topo.may_write(c, 8 * d + RANK_CORE)]
+        h = min(pool, key=lambda c: (work.get(c, 0), topo.may_write(c, (c ^ 8)), c))
+        work[h] = work.get(h, 0) + 1
+        slot = inbound.get(h, 0)
+        inbound[h] = slot + 1
+        sends.setdefault(8 * s + RANK_CORE, []).append((h, d, slot))
+        sends.setdefault(h, []).append((8 * d + RANK_CORE, slot, s))
+    for r in range(N):
+        inbound[8 * r + RANK_CORE] = N - 1
+    return sends, inbound
+
+
+def issue(g, core, T, topo, src_buf, todo):
+    off = [w for w in todo if w[0] // 8 != core // 8]
+    on = [w for w in todo if w[0] // 8 == core // 8]
+    calls = max((len(off) + 7) // 8, (len(todo) + 15) // 16)
+    for i in range(calls):
+        batch = off[i::calls] + on[i::calls]
+        transfers = []
+        for e, (dst, a, b) in enumerate(batch):
+            rid, pid = topo.addr(dst, core)
+            transfers.append(RemoteDMATransfer(dst_ids=[DstId(rid=rid, pnc=pid)], dma_engine_mask=1 << e,
+                                               remote_sem=T.sem.arrived, src=src_buf[:, B * a:B * a + B],
+                                               dst=T.land[:, B * b:B * b + B]))
+        g.remote_dma_fused(transfers, local_sem=T.sem.sent)
+    return len(todo)
+
+
+def rank_program(g, core, T, topo):
+    if "plan" not in CACHE:
+        CACHE["plan"] = plan(T.tables["DEAD"], topo)
+    sends, inbound = CACHE["plan"]
+    rank = T.rank_of(core)
+    if rank is None:
+        if core not in sends:
+            return
+        g.wait_ge(T.sem.arrived, inbound[core])
+        n = issue(g, core, T, topo, T.land, sends[core])
+        g.wait_ge(T.sem.sent, n)
+        return
+    own = slice(B * rank, B * rank + B)
+    g.dma_start(T.xs[:], T.x[:]).then_inc(T.sem.loaded, 16)
+    g.dma_start(T.land[:, own], T.x[:, own]).then_inc(T.sem.loaded, 16)
+    g.wait_ge(T.sem.loaded, 32)
+    n = issue(g, core, T, topo, T.xs, sends[core])
+    g.wait_ge(T.sem.sent, n)
+    g.wait_ge(T.sem.arrived, inbound[core])
+    g.dma_start(T.y[:], T.land[:]).then_inc(T.sem.stored, 16)
+    g.wait_ge(T.sem.stored, 16)

@@ -1,9 +1,11 @@
-import math
 from concourse.bass import DstId, RemoteDMATransfer
 
 N = 32
 B = 16
 RANK_CORE = 3
+RUN = 8
+CHIP_BLOCKS = 33
+AIM = {"out": 28, "in": 28, "mate": 13}
 
 SCRATCH = {
     "xs": ("sbuf", [128, 512], "float32"),
@@ -32,89 +34,126 @@ def plan(dead, topo):
             links.append(("in", b, die))
         return links
 
-    def candidates(s, d):
-        out = []
-        for die in (1, 0):
-            w = way(s, die, d)
-            if w is not None:
-                out.append(((s, die), w + [("leave", s), ("enter", d)] + ([("die0", s)] if die == 0 else [])))
-        for m in range(N):
-            if m in (s, d) or (s // 16 == d // 16 and m // 16 != s // 16):
-                continue
-            w1 = way(s, 1, m)
-            if w1 is None:
-                continue
-            for die in (1, 0):
-                w2 = way(m, die, d)
-                if w2 is not None:
-                    out.append(((m, die), w1 + w2 + [("leave", s), ("enter", m), ("leave", m), ("enter", d), ("relayed", s)]))
-        return out
+    def whole(c):
+        return all((c & ~1, d) not in dead_mate and (c, d) not in dead_port and (c ^ 1, d) not in dead_port for d in (0, 1))
 
-    cand = {(s, d): candidates(s, d) for s in range(N) for d in range(N) if s != d}
-    cap = {"leave": 33, "enter": 33, "out": 30, "in": 30, "mate": 16, "die0": 16, "relayed": 16}
+    def detour(s, m, d):
+        return s // 16 == d // 16 != m // 16
+
+    def reaches(s, die, dests):
+        return all(way(s, die, d) is not None for d in dests)
+
+    segs = {}
+    for s in range(N):
+        stuck = [d for d in range(N) if d != s and not reaches(s, 0, [d]) and not reaches(s, 1, [d])]
+        if len(stuck) > 8:
+            best = {N: (0, [])}
+            for p in range(N - 1, -1, -1):
+                if p == s:
+                    best[p] = best[p + 1]
+                    continue
+                best[p] = (best[p + 1][0] + 1, [(p, 1)] + best[p + 1][1])
+                c = p + 1
+                if (p + 3 <= N and not p <= s < p + 3 and (c ^ s) & 1 == 0 and whole(c) and way(s, 1, c) is not None
+                        and not detour(s, c, p) and not detour(s, c, p + 2) and best[p + 3][0] + 1 < best[p][0]):
+                    best[p] = (best[p + 3][0] + 1, [(p, 3)] + best[p + 3][1])
+            segs[s] = best[0][1]
+        else:
+            runs = []
+            for k in range(1, 4):
+                g = (s // RUN + k) % 4
+                if len(runs) < 2 and any(reaches(s, die, range(RUN * g, RUN * g + RUN)) for die in (0, 1)):
+                    runs.append(g)
+            segs[s] = [(RUN * g, RUN) for g in runs] + [(d, 1) for d in range(N) if d != s and d // RUN not in runs]
+
+    def forward(m, die, dests):
+        use = []
+        kind = ("owner%d" % die) if any((m ^ d) & 1 for d in dests) else "other"
+        for d in dests:
+            if d != m:
+                use += [(l, 1) for l in way(m, die, d)] + [(("leave", m), 1), (("enter", d), 1), ((kind, m, die), 1)]
+        return use
+
+    cand = {}
+    for s in range(N):
+        for a, n in segs[s]:
+            dests, out = list(range(a, a + n)), []
+            if n == 1 and reaches(s, 1, dests):
+                out.append(((a, None), [(l, 1) for l in way(s, 1, a)] + [(("leave", s), 1), (("enter", a), 1), (("off", s, n), 1)]))
+            for die in (1, 0):
+                if reaches(s, die, dests):
+                    out.append(((s, die), forward(s, die, dests) + [(("on", s, n), 1)]))
+            for m in ([a + 1] if n == 3 else range(N) if n == 1 else []):
+                if m == s or (n == 1 and m == a) or way(s, 1, m) is None or any(detour(s, m, d) for d in dests):
+                    continue
+                for die in (1, 0):
+                    if reaches(m, die, [d for d in dests if d != m]):
+                        out.append(((m, die), [(l, n) for l in way(s, 1, m)] + forward(m, die, dests)
+                                    + [(("leave", s), n), (("enter", m), n), (("off", s, n), 1), (("relay",), 1)]))
+            cand[(s, a, n)] = out
+
+    limit = {"leave": CHIP_BLOCKS, "enter": CHIP_BLOCKS, "off": 8, "on": 8, "owner1": 16, "owner0": 32, "other": 32}
     load = {}
 
-    def cost(res):
-        c = 0.0
-        for r in res:
-            n, k = load.get(r, 0) + 1, cap[r[0]]
-            c += (n / k) ** 6 + (1000.0 * (n - k) if n > k else 0.0)
-        return c
+    def price(kind, x):
+        if kind in limit:
+            return 1e6 * (x - limit[kind]) if x > limit[kind] else 0.0
+        if kind == "relay":
+            return 0.3 * x
+        return 1e-3 * x * x + ((x - AIM[kind]) ** 2 if x > AIM[kind] else 0.0)
 
-    keys = sorted(cand, key=lambda k: (len(cand[k]), k))
+    def cost(use):
+        return sum(price(r[0], load.get(r, 0) + n) - price(r[0], load.get(r, 0)) for r, n in use)
+
+    keys = sorted(cand, key=lambda k: (-k[2], len(cand[k]), k))
     choice = {}
     for sweep in range(12):
         for k in keys:
             if k in choice:
-                for r in cand[k][choice[k]][1]:
-                    load[r] -= 1
+                for r, n in cand[k][choice[k]][1]:
+                    load[r] -= n
             choice[k] = min(range(len(cand[k])), key=lambda i: (cost(cand[k][i][1]), i))
-            for r in cand[k][choice[k]][1]:
-                load[r] = load.get(r, 0) + 1
+            for r, n in cand[k][choice[k]][1]:
+                load[r] = load.get(r, 0) + n
+    assert all(x <= limit[r[0]] for r, x in load.items() if r[0] in limit)
 
-    direct = {s: 0 for s in range(N)}
-    jobs = {}
-    sends, inbound = {}, {}
-    for (s, d) in keys:
-        m, die = cand[(s, d)][choice[(s, d)]][0]
-        if m != s:
-            direct[s] += 1
-    hop = []
-    for (s, d) in sorted(keys):
-        m, die = cand[(s, d)][choice[(s, d)]][0]
-        if m == s and die == 1 and direct[s] < 16:
-            direct[s] += 1
-            sends.setdefault(8 * s + RANK_CORE, []).append((8 * d + RANK_CORE, d, s))
-        else:
-            hop.append(((m ^ d) & 1 == 0, s, d, m, die))
-    work = {}
-    for same, s, d, m, die in sorted(hop):
+    sends, inbound, held, busy = {}, {}, {}, {}
+    for s, a, n in keys:
+        m, die = cand[(s, a, n)][choice[(s, a, n)]][0]
+        src = 8 * s + RANK_CORE
+        if die is None:
+            sends.setdefault(src, []).append((8 * a + RANK_CORE, a, 1, s))
+            continue
         pool = [c for c in range(8 * m, 8 * m + 8) if c % 8 != RANK_CORE and topo.die(c) == die
-                and topo.may_write(c, 8 * d + RANK_CORE)]
-        h = min(pool, key=lambda c: (work.get(c, 0), topo.may_write(c, (c ^ 8)), c))
-        work[h] = work.get(h, 0) + 1
-        slot = inbound.get(h, 0)
-        inbound[h] = slot + 1
-        sends.setdefault(8 * s + RANK_CORE, []).append((h, d, slot))
-        sends.setdefault(h, []).append((8 * d + RANK_CORE, slot, s))
+                and all(topo.may_write(c, 8 * d + RANK_CORE) for d in range(a, a + n))]
+        h = min(pool, key=lambda c: (busy.get(c, 0), topo.may_write(c, c ^ 8), c))
+        busy[h] = busy.get(h, 0) + n
+        slot = held.get(h, 0)
+        held[h] = slot + n
+        inbound[h] = inbound.get(h, 0) + 1
+        sends.setdefault(src, []).append((h, a, n, slot))
+        for i in range(n):
+            sends.setdefault(h, []).append((8 * (a + i) + RANK_CORE, slot + i, 1, s))
     for r in range(N):
         inbound[8 * r + RANK_CORE] = N - 1
     return sends, inbound
 
 
 def issue(g, core, T, topo, src_buf, todo):
-    off = [w for w in todo if w[0] // 8 != core // 8]
-    on = [w for w in todo if w[0] // 8 == core // 8]
-    calls = max((len(off) + 7) // 8, (len(todo) + 15) // 16)
-    for i in range(calls):
-        batch = off[i::calls] + on[i::calls]
-        transfers = []
-        for e, (dst, a, b) in enumerate(batch):
-            rid, pid = topo.addr(dst, core)
-            transfers.append(RemoteDMATransfer(dst_ids=[DstId(rid=rid, pnc=pid)], dma_engine_mask=1 << e,
-                                               remote_sem=T.sem.arrived, src=src_buf[:, B * a:B * a + B],
-                                               dst=T.land[:, B * b:B * b + B]))
-        g.remote_dma_fused(transfers, local_sem=T.sem.sent)
+    for width in sorted({w[2] for w in todo}, reverse=True):
+        off = [w for w in todo if w[2] == width and w[0] // 8 != core // 8]
+        on = [w for w in todo if w[2] == width and w[0] // 8 == core // 8]
+        while off or on:
+            batch, off = off[:8], off[8:]
+            k = 16 - len(batch)
+            batch, on = batch + on[:k], on[k:]
+            transfers = []
+            for e, (dst, a, n, b) in enumerate(batch):
+                rid, pid = topo.addr(dst, core)
+                transfers.append(RemoteDMATransfer(dst_ids=[DstId(rid=rid, pnc=pid)], dma_engine_mask=1 << e,
+                                                   remote_sem=T.sem.arrived, src=src_buf[:, B * a:B * (a + n)],
+                                                   dst=T.land[:, B * b:B * (b + n)]))
+            g.remote_dma_fused(transfers, local_sem=T.sem.sent)
     return len(todo)
 
 

@@ -97,10 +97,10 @@ def plan(dead, topo):
 
     def price(kind, x):
         if kind in limit:
-            return 1e6 * (x - limit[kind]) if x > limit[kind] else 0.0
+            return 10 ** 9 * max(0, x - limit[kind])
         if kind == "relay":
-            return 0.3 * x
-        return 1e-3 * x * x + ((x - AIM[kind]) ** 2 if x > AIM[kind] else 0.0)
+            return 300 * x
+        return x * x + 1000 * max(0, x - AIM[kind]) ** 2
 
     def cost(use):
         return sum(price(r[0], load.get(r, 0) + n) - price(r[0], load.get(r, 0)) for r, n in use)
@@ -117,7 +117,7 @@ def plan(dead, topo):
                 load[r] = load.get(r, 0) + n
     assert all(x <= limit[r[0]] for r, x in load.items() if r[0] in limit)
 
-    sends, inbound, held, busy = {}, {}, {}, {}
+    sends, inbound, held = {}, {}, {}
     for s, a, n in keys:
         m, die = cand[(s, a, n)][choice[(s, a, n)]][0]
         src = 8 * s + RANK_CORE
@@ -126,14 +126,14 @@ def plan(dead, topo):
             continue
         pool = [c for c in range(8 * m, 8 * m + 8) if c % 8 != RANK_CORE and topo.die(c) == die
                 and all(topo.may_write(c, 8 * d + RANK_CORE) for d in range(a, a + n))]
-        h = min(pool, key=lambda c: (busy.get(c, 0), topo.may_write(c, c ^ 8), c))
-        busy[h] = busy.get(h, 0) + n
+        h = min(pool, key=lambda c: (held.get(c, 0), topo.may_write(c, c ^ 8), c))
         slot = held.get(h, 0)
         held[h] = slot + n
         inbound[h] = inbound.get(h, 0) + 1
         sends.setdefault(src, []).append((h, a, n, slot))
         for i in range(n):
             sends.setdefault(h, []).append((8 * (a + i) + RANK_CORE, slot + i, 1, s))
+    assert all(n <= 16 for n in held.values())
     for r in range(N):
         inbound[8 * r + RANK_CORE] = N - 1
     return sends, inbound

from concourse.bass import DstId, RemoteDMATransfer

N = 32
B = 16
RANK_CORE = 3
RUN = 8
CHIP_BLOCKS = 33
AIM = {"out": 28, "in": 28, "mate": 13}

SCRATCH = {
    "xs": ("sbuf", [128, 512], "float32"),
    "land": ("sbuf", [128, 512], "float32"),
}
SEMAPHORES = ["loaded", "arrived", "sent", "stored"]

CACHE = {}


def plan(dead, topo):
    dead_mate = {(c & ~1, d) for c, d in dead["mate_links"]}
    dead_port = {(c, d) for c, d in dead["switch_ports"]}

    def way(a, die, b):
        links, cur = [], a
        if (a ^ b) & 1:
            if (cur & ~1, die) in dead_mate:
                return None
            links.append(("mate", cur, die))
            cur ^= 1
        if cur != b:
            if (cur, die) in dead_port or (b, die) in dead_port:
                return None
            links.append(("out", cur, die))
            links.append(("in", b, die))
        return links

    def whole(c):
        return all((c & ~1, d) not in dead_mate and (c, d) not in dead_port and (c ^ 1, d) not in dead_port for d in (0, 1))

    def detour(s, m, d):
        return s // 16 == d // 16 != m // 16

    def reaches(s, die, dests):
        return all(way(s, die, d) is not None for d in dests)

    segs = {}
    for s in range(N):
        stuck = [d for d in range(N) if d != s and not reaches(s, 0, [d]) and not reaches(s, 1, [d])]
        if len(stuck) > 8:
            best = {N: (0, [])}
            for p in range(N - 1, -1, -1):
                if p == s:
                    best[p] = best[p + 1]
                    continue
                best[p] = (best[p + 1][0] + 1, [(p, 1)] + best[p + 1][1])
                c = p + 1
                if (p + 3 <= N and not p <= s < p + 3 and (c ^ s) & 1 == 0 and whole(c) and way(s, 1, c) is not None
                        and not detour(s, c, p) and not detour(s, c, p + 2) and best[p + 3][0] + 1 < best[p][0]):
                    best[p] = (best[p + 3][0] + 1, [(p, 3)] + best[p + 3][1])
            segs[s] = best[0][1]
        else:
            runs = []
            for k in range(1, 4):
                g = (s // RUN + k) % 4
                if len(runs) < 2 and any(reaches(s, die, range(RUN * g, RUN * g + RUN)) for die in (0, 1)):
                    runs.append(g)
            segs[s] = [(RUN * g, RUN) for g in runs] + [(d, 1) for d in range(N) if d != s and d // RUN not in runs]

    def forward(m, die, dests):
        use = []
        kind = ("owner%d" % die) if any((m ^ d) & 1 for d in dests) else "other"
        for d in dests:
            if d != m:
                use += [(l, 1) for l in way(m, die, d)] + [(("leave", m), 1), (("enter", d), 1), ((kind, m, die), 1)]
        return use

    cand = {}
    for s in range(N):
        for a, n in segs[s]:
            dests, out = list(range(a, a + n)), []
            if n == 1 and reaches(s, 1, dests):
                out.append(((a, None), [(l, 1) for l in way(s, 1, a)] + [(("leave", s), 1), (("enter", a), 1), (("off", s, n), 1)]))
            for die in (1, 0):
                if reaches(s, die, dests):
                    out.append(((s, die), forward(s, die, dests) + [(("on", s, n), 1)]))
            for m in ([a + 1] if n == 3 else range(N) if n == 1 else []):
                if m == s or (n == 1 and m == a) or way(s, 1, m) is None or any(detour(s, m, d) for d in dests):
                    continue
                for die in (1, 0):
                    if reaches(m, die, [d for d in dests if d != m]):
                        out.append(((m, die), [(l, n) for l in way(s, 1, m)] + forward(m, die, dests)
                                    + [(("leave", s), n), (("enter", m), n), (("off", s, n), 1), (("relay",), 1)]))
            cand[(s, a, n)] = out

    limit = {"leave": CHIP_BLOCKS, "enter": CHIP_BLOCKS, "off": 8, "on": 8, "owner1": 16, "owner0": 32, "other": 32}
    load = {}

    def price(kind, x):
        if kind in limit:
            return 10 ** 9 * max(0, x - limit[kind])
        if kind == "relay":
            return 300 * x
        return x * x + 1000 * max(0, x - AIM[kind]) ** 2

    def cost(use):
        return sum(price(r[0], load.get(r, 0) + n) - price(r[0], load.get(r, 0)) for r, n in use)

    keys = sorted(cand, key=lambda k: (-k[2], len(cand[k]), k))
    choice = {}
    for sweep in range(12):
        for k in keys:
            if k in choice:
                for r, n in cand[k][choice[k]][1]:
                    load[r] -= n
            choice[k] = min(range(len(cand[k])), key=lambda i: (cost(cand[k][i][1]), i))
            for r, n in cand[k][choice[k]][1]:
                load[r] = load.get(r, 0) + n
    assert all(x <= limit[r[0]] for r, x in load.items() if r[0] in limit)

    sends, inbound, held = {}, {}, {}
    for s, a, n in keys:
        m, die = cand[(s, a, n)][choice[(s, a, n)]][0]
        src = 8 * s + RANK_CORE
        if die is None:
            sends.setdefault(src, []).append((8 * a + RANK_CORE, a, 1, s))
            continue
        pool = [c for c in range(8 * m, 8 * m + 8) if c % 8 != RANK_CORE and topo.die(c) == die
                and all(topo.may_write(c, 8 * d + RANK_CORE) for d in range(a, a + n))]
        h = min(pool, key=lambda c: (held.get(c, 0), topo.may_write(c, c ^ 8), c))
        slot = held.get(h, 0)
        held[h] = slot + n
        inbound[h] = inbound.get(h, 0) + 1
        sends.setdefault(src, []).append((h, a, n, slot))
        for i in range(n):
            sends.setdefault(h, []).append((8 * (a + i) + RANK_CORE, slot + i, 1, s))
    assert all(n <= 16 for n in held.values())
    for r in range(N):
        inbound[8 * r + RANK_CORE] = N - 1
    return sends, inbound


def issue(g, core, T, topo, src_buf, todo):
    for width in sorted({w[2] for w in todo}, reverse=True):
        off = [w for w in todo if w[2] == width and w[0] // 8 != core // 8]
        on = [w for w in todo if w[2] == width and w[0] // 8 == core // 8]
        while off or on:
            batch, off = off[:8], off[8:]
            k = 16 - len(batch)
            batch, on = batch + on[:k], on[k:]
            transfers = []
            for e, (dst, a, n, b) in enumerate(batch):
                rid, pid = topo.addr(dst, core)
                transfers.append(RemoteDMATransfer(dst_ids=[DstId(rid=rid, pnc=pid)], dma_engine_mask=1 << e,
                                                   remote_sem=T.sem.arrived, src=src_buf[:, B * a:B * (a + n)],
                                                   dst=T.land[:, B * b:B * (b + n)]))
            g.remote_dma_fused(transfers, local_sem=T.sem.sent)
    return len(todo)


def rank_program(g, core, T, topo):
    if "plan" not in CACHE:
        CACHE["plan"] = plan(T.tables["DEAD"], topo)
    sends, inbound = CACHE["plan"]
    rank = T.rank_of(core)
    if rank is None:
        if core not in sends:
            return
        g.wait_ge(T.sem.arrived, inbound[core])
        n = issue(g, core, T, topo, T.land, sends[core])
        g.wait_ge(T.sem.sent, n)
        return
    own = slice(B * rank, B * rank + B)
    g.dma_start(T.xs[:], T.x[:]).then_inc(T.sem.loaded, 16)
    g.dma_start(T.land[:, own], T.x[:, own]).then_inc(T.sem.loaded, 16)
    g.wait_ge(T.sem.loaded, 32)
    n = issue(g, core, T, topo, T.xs, sends[core])
    g.wait_ge(T.sem.sent, n)
    g.wait_ge(T.sem.arrived, inbound[core])
    g.dma_start(T.y[:], T.land[:]).then_inc(T.sem.stored, 16)
    g.wait_ge(T.sem.stored, 16)
